import numpy as np
import ml_dtypes


def mxq(x, axis, fmt="e4m3"):
    dtype, down = {"e4m3": (ml_dtypes.float8_e4m3fn, 7), "e5m2": (ml_dtypes.float8_e5m2, 14)}[fmt]
    v = np.moveaxis(np.asarray(x, np.float32).astype(ml_dtypes.bfloat16).astype(np.float64), axis, -1)
    blocks = v.reshape(v.shape[:-1] + (-1, 32))
    amax = np.abs(blocks).max(-1, keepdims=True)
    byte = np.maximum(np.where(amax > 0, np.frexp(amax)[1] - 1 + 127, 0) - down, 1)
    scale = np.exp2(byte - 127.0)
    codes = (blocks / scale).astype(np.float32).astype(dtype).astype(np.float64)
    return np.moveaxis((codes * scale).reshape(v.shape), -1, axis)


WIDE = False


def mx_kscale(k):
    if not WIDE:
        return np.ones(k)
    levels = np.array([10, -10, 5, -5, 0])
    if k % 512:
        return np.exp2(np.random.permutation(np.resize(levels, k // 32))).repeat(32)
    a = np.empty((k // 512, 16))
    for p in range(k // 512):
        a[p, :8] = np.random.permutation(np.resize(levels, 8))
        for g in range(8):
            far = levels[np.abs(levels - a[p, g]) >= 10]
            a[p, g + 8] = far[np.random.randint(len(far))]
    return np.exp2(a.ravel()).repeat(32)


def f64(x):
    return np.asarray(x).astype(np.float64)


def striped(idx):
    return np.tile(idx.reshape(-1, 16).T, (8, 1)).astype(np.uint16)


def unstriped(offs):
    return offs[:16].T.reshape(-1).astype(np.int64)


def striped8(idx):
    return np.concatenate([x.reshape(-1, 16).T for x in idx]).astype(np.uint16)


def runs(offs, k):
    lists = np.stack([offs[16 * r : 16 * r + 16].T.reshape(-1) for r in range(8)]).astype(np.int64)
    return lists[np.arange(k) % 512 // 64]


def pack_weight(w):
    k, n = w.shape
    w = f64(np.asarray(w, np.float32).astype(ml_dtypes.bfloat16)).reshape(k // 32, 32, n)
    amax = np.abs(w).max(1)
    byte = np.clip(np.where(amax > 0, np.frexp(amax)[1] - 1 + 127 - 7, 1), 1, 254)
    scaled = (w * np.exp2(127.0 - byte)[:, None, :]).reshape(k, n).astype(np.float32)
    words = np.ascontiguousarray(scaled.reshape(k // 512, 128, 4, n).transpose(0, 1, 3, 2)).astype(ml_dtypes.float8_e4m3fn).view(np.uint8)
    return words, np.ascontiguousarray(byte.astype(np.uint8).reshape(k // 512, 16, n))


def unpack_weight(words, scales):
    g, p, n, _ = words.shape
    vals = np.ascontiguousarray(words).view(ml_dtypes.float8_e4m3fn).astype(np.float64) * np.repeat(np.exp2(scales.astype(np.float64) - 127.0), 8, axis=1)[..., None]
    return vals.transpose(0, 1, 3, 2).reshape(g * 512, n)


E2M1 = np.array([0.0, 0.5, 1.0, 1.5, 2.0, 3.0, 4.0, 6.0, -0.0, -0.5, -1.0, -1.5, -2.0, -3.0, -4.0, -6.0])


def pack_fp4(w):
    k, n = w.shape
    w = f64(np.asarray(w, np.float32).astype(ml_dtypes.bfloat16)).reshape(k // 32, 32, n)
    amax = np.abs(w).max(1)
    mant, ex = np.frexp(amax / 6.0)
    byte = np.clip(np.where(amax > 0, np.where(mant > 0.5, ex, ex - 1) + 127, 1), 1, 254)
    scaled = (w * np.exp2(127.0 - byte)[:, None, :]).reshape(k, n).astype(np.float32)
    c = np.ascontiguousarray(scaled.reshape(k // 512, 128, 4, n).transpose(0, 1, 3, 2)).astype(ml_dtypes.float4_e2m1fn).view(np.uint8) & 0xF
    words = (c[..., 0::2] | (c[..., 1::2] << 4)).reshape(k // 512, 128, 2 * n)
    return np.ascontiguousarray(words), np.ascontiguousarray(byte.astype(np.uint8).reshape(k // 512, 16, n))


def unpack_fp4(words, scales):
    g, _, n = scales.shape
    words = np.ascontiguousarray(words).reshape(g, 128, n, 2)
    nib = np.empty((g, 128, n, 4), np.uint8)
    nib[..., 0::2] = words & 0xF
    nib[..., 1::2] = words >> 4
    vals = E2M1[nib] * np.repeat(np.exp2(scales.astype(np.float64) - 127.0), 8, axis=1)[..., None]
    return vals.transpose(0, 1, 3, 2).reshape(g * 512, n)


def sigmoid(v):
    return 1.0 / (1.0 + np.exp(-np.maximum(v, -700.0)))

def planes(y):
    n, m = y.shape
    v = y.astype(np.float32).astype(ml_dtypes.bfloat16).astype(np.float64).reshape(n // 32, 32, m)
    top = np.abs(v).max(1)
    byte = np.clip(np.where(top > 0, np.frexp(top)[1] - 1 + 127 - 7, 1), 1, 254)
    codes = (v * np.exp2(127.0 - byte)[:, None, :]).reshape(n, m).astype(np.float32).astype(ml_dtypes.float8_e4m3fn).view(np.uint8)
    words = codes.reshape(n // 512, 128, 4, m).transpose(0, 1, 3, 2)
    return np.ascontiguousarray(words), np.ascontiguousarray(byte.astype(np.uint8).reshape(n // 512, 16, m))


K, T, S, H, C, W = 512, 2048, 512, 512, 512, 256


def setup_inputs():
    n = np.random.standard_normal
    s = mx_kscale(K)[:, None]
    packed_xT = pack_weight(n((K, T)) * s)
    packed_w1 = pack_fp4(n((K, H)) / np.sqrt(K) / s)
    packed_w2 = pack_fp4(n((K, H)) / np.sqrt(K) / s)
    perm = np.stack([np.random.permutation(S) for _ in range(8)])
    return {
        "x_words": packed_xT[0],
        "x_scales": packed_xT[1],
        "w1_words": packed_w1[0],
        "w1_scales": packed_w1[1],
        "w2_words": packed_w2[0],
        "w2_scales": packed_w2[1],
        "gs": (np.random.uniform(0.5, 1.5, (K, 1)) / s).astype(np.float32),
        "offs": striped(np.random.permutation(T)[:S]),
        "two": striped(np.random.permutation(T)[:S]),
        "n1": striped8(np.stack([np.random.permutation(S) for _ in range(8)])),
        "n2": striped8(np.stack([np.random.permutation(S) for _ in range(8)])),
        "cand": striped(np.random.permutation(T)[:C]),
        "n3": striped8(perm[:, :W]),
        "n4": striped8(perm[:, W:]),
    }


def reference(x_words, x_scales, w1_words, w1_scales, w2_words, w2_scales, gs, offs, two, n1, n2, cand, n3, n4):
    x_cand = unpack_weight(x_words, x_scales)[:, unstriped(cand)]
    xq = unpack_weight(x_words, x_scales)[:, unstriped(offs)]
    y = unpack_fp4(w1_words, w1_scales).T @ xq
    x_two = unpack_weight(x_words, x_scales)[:, unstriped(two)]
    d = unpack_fp4(w2_words, w2_scales).T @ x_two
    z = f64(gs) * ((y + y[np.arange(H)[:, None], runs(n1, H)]) * (sigmoid(d + d[np.arange(H)[:, None], runs(n2, H)])))
    s = 0.0625 * ((x_cand.T @ mxq(z, 0, "e4m3")))
    pb = s[np.arange(C)[:, None], runs(n4, C)]
    pa = s[np.arange(C)[:, None], runs(n3, C)]
    rb = pb - (0.5 * pa)
    ra = np.sqrt((pa) ** 2 + (pb) ** 2 + 0.25)
    ds = np.zeros((C, S))
    ds[np.arange(C)[:, None], runs(n3, C)] = ra
    out = ds.copy()
    out[np.arange(C)[:, None], runs(n4, C)] = rb
    return (out,) + planes(out)

@@ -1,0 +1,199 @@
+from contextlib import ExitStack
+
+import concourse.mybir as mybir
+
+F32 = mybir.dt.float32
+BF16 = mybir.dt.bfloat16
+I32 = mybir.dt.int32
+U32 = mybir.dt.uint32
+U16 = mybir.dt.uint16
+U8 = mybir.dt.uint8
+FP8X4 = mybir.dt.float8_e4m3fn_x4
+FP4X4 = mybir.dt.float4_e2m1fn_x4
+ACT = mybir.ActivationFunctionType
+ALU = mybir.AluOpType
+
+P = 128
+PACK = 4
+T = 2048
+S = 512
+W = 256
+HALF = S // 2
+FLOPS = 3 * 2 * 512 * 512 * 512
+
+
+def tile_picked_twctriebpolar_none_po_kernel(tc, x_words, x_scales, w1_words, w1_scales, w2_words, w2_scales, gs, offs, two, n1, n2, cand, n3, n4, out_0, out_1, out_2):
+    nc = tc.nc
+    with ExitStack() as ctx:
+        held = ctx.enter_context(tc.tile_pool(name="held", bufs=1))
+        psum = ctx.enter_context(tc.psum_pool(name="psum", bufs=8))
+
+        def sb(name, shape, dtype):
+            return held.tile(shape, dtype, name=name, align_bytes=64)
+
+        def load_list(name, src):
+            tile = held.tile(list(src.shape), U16, name=name)
+            nc.sync.dma_start(tile[:], src)
+            return tile
+
+        def load_scales(tile, src):
+            for q in range(4):
+                nc.sync.dma_start(tile[32 * q : 32 * q + 4, :].bitcast(I32), src[0, 4 * q : 4 * q + 4, :].bitcast(I32))
+
+        xs = sb("xs", [P, T], U8)
+        w2s_raw = sb("w2s_raw", [P, S], U8)
+        w1s_raw = sb("w1s_raw", [P, S], U8)
+        for tile in (xs, w2s_raw, w1s_raw):
+            nc.vector.memset(tile[:].bitcast(I32), 0)
+
+        xw = sb("xw", [P, T], U32)
+        w2w_raw = sb("w2w_raw", [P, 2 * S], U8)
+        w1w_raw = sb("w1w_raw", [P, 2 * S], U8)
+        gain = sb("gain", [P, PACK], F32)
+
+        load_scales(xs, x_scales)
+        two_l = load_list("two_l", two)
+        nc.sync.dma_start(w2w_raw[:].bitcast(I32), w2_words[0].bitcast(I32))
+        nc.sync.dma_start(xw[:].bitcast(I32), x_words[0].rearrange("p n t -> p (n t)").bitcast(I32))
+        load_scales(w2s_raw, w2_scales)
+        offs_l = load_list("offs_l", offs)
+        nc.sync.dma_start(w1w_raw[:].bitcast(I32), w1_words[0].bitcast(I32))
+        load_scales(w1s_raw, w1_scales)
+        n2_l = load_list("n2_l", n2)
+        nc.sync.dma_start(gain[:], gs.rearrange("(p t) o -> p (t o)", t=PACK))
+        n1_l = load_list("n1_l", n1)
+        cand_l = load_list("cand_l", cand)
+        n3_l = load_list("n3_l", n3)
+        n4_l = load_list("n4_l", n4)
+
+        def deal_words(name, raw):
+            dealt = sb(name, [P, 2 * S], U8)
+            nc.vector.tensor_copy(dealt[:].rearrange("p (t m b) -> p t m b", t=PACK, b=2), raw[:].rearrange("p (m t b) -> p t m b", t=PACK, b=2))
+            return dealt
+
+        def deal_scales(name, raw):
+            dealt = sb(name, [P, S], U8)
+            nc.vector.tensor_copy(dealt[:].rearrange("p (t m) -> p t m", t=PACK), raw[:].rearrange("p (m t) -> p t m", t=PACK))
+            return dealt
+
+        def pick_scales(name, offsets):
+            picked = sb(name, [P, S], U8)
+            nc.vector.tensor_copy(picked[:], xs[:].indirect(offsets[:]))
+            return picked
+
+        def pick_words(name, offsets):
+            picked = sb(name, [P, S], U32)
+            nc.vector.tensor_copy(picked[:], xw[:].indirect(offsets[:]))
+            return picked
+
+        def project(name, ww, ws, words, scales, row_scale):
+            windows = [sb("%s_win%d" % (name, t), [P, 2 * S], F32) for t in range(PACK)]
+            for t in range(PACK):
+                bank = psum.tile([P, S], F32, name="bank")
+                nc.tensor.matmul_mx(bank[:], lhsT=ww[:, 2 * P * t : 2 * P * (t + 1)].bitcast(FP4X4), lhsT_scale=ws[:, P * t : P * (t + 1)],
+                                    rhs=words[:].bitcast(FP8X4), rhs_scale=scales[:], start=True, stop=True)
+                scale = 1.0 if row_scale is None else row_scale[:, t : t + 1]
+                nc.scalar.activation(windows[t][:, :S], bank[:], ACT.Copy, scale=scale)
+                nc.scalar.activation(windows[t ^ 1][:, S:], bank[:], ACT.Copy, scale=scale)
+            return windows
+
+        two_s = pick_scales("two_s", two_l)
+        w2w = deal_words("w2w", w2w_raw)
+        two_w = pick_words("two_w", two_l)
+        w2s = deal_scales("w2s", w2s_raw)
+        d_win = project("d", w2w, w2s, two_w, two_s, None)
+
+        offs_w = pick_words("offs_w", offs_l)
+        offs_s = pick_scales("offs_s", offs_l)
+        w1w = deal_words("w1w", w1w_raw)
+        w1s = deal_scales("w1s", w1s_raw)
+        y_win = project("y", w1w, w1s, offs_w, offs_s, gain)
+
+        cand_s_raw = pick_scales("cand_s_raw", cand_l)
+
+        gate = sb("gate", [P, PACK, S], F32)
+        ysum = sb("ysum", [P, PACK, S], F32)
+        for t in range(PACK):
+            dsum = sb("dsum%d" % t, [P, S], F32)
+            nc.vector.tensor_tensor(dsum[:], d_win[t][:].indirect(n2_l[:]), d_win[t ^ 1][:, S:], ALU.add)
+            nc.scalar.activation(gate[:, t, :], dsum[:], ACT.Sigmoid)
+        for t in range(PACK):
+            nc.vector.tensor_tensor(ysum[:, t, :], y_win[t][:].indirect(n1_l[:]), y_win[t ^ 1][:, S:], ALU.add)
+
+        cand_w = sb("cand_w", [P, S], U32)
+        nc.vector.tensor_copy(cand_w[:].rearrange("p (t m) -> p m t", t=PACK), xw[:].indirect(cand_l[:]))
+        z_half = []
+        for h in range(2):
+            cols = slice(h * HALF, (h + 1) * HALF)
+            z = sb("z%d" % h, [P, HALF, PACK], BF16)
+            nc.vector.tensor_tensor(z[:].rearrange("p (c i) t -> p c t i", i=4), ysum[:, :, cols].rearrange("p t (c i) -> p c t i", i=4),
+                                    gate[:, :, cols].rearrange("p t (c i) -> p c t i", i=4), ALU.mult)
+            z_half.append(z)
+        cand_s = deal_scales("cand_s", cand_s_raw)
+        z_w = []
+        z_s = []
+        for h in range(2):
+            z_w.append(sb("z_w%d" % h, [P, HALF], U32))
+            z_s.append(sb("z_s%d" % h, [P, HALF], U8))
+            nc.vector.quantize_mx(z_w[h][:].bitcast(FP8X4), z_s[h][:], z_half[h][:].rearrange("p c t -> p (c t)"))
+
+        score = [sb("score%d" % t, [P, S], F32) for t in range(PACK)]
+        for t in range(PACK):
+            for h in range(2):
+                bank = psum.tile([P, S], F32, name="bank")
+                nc.tensor.matmul_mx(bank[:, :HALF], lhsT=cand_w[:, P * t : P * (t + 1)].bitcast(FP8X4), lhsT_scale=cand_s[:, P * t : P * (t + 1)],
+                                    rhs=z_w[h][:].bitcast(FP8X4), rhs_scale=z_s[h][:], start=True, stop=True)
+                nc.scalar.activation(score[t][:, h * HALF : (h + 1) * HALF], bank[:, :HALF], ACT.Copy, scale=0.0625)
+
+        pairs = [sb("pairs%d" % t, [P, 2 * W], F32) for t in range(PACK)]
+        squares = [sb("squares%d" % t, [P, 2 * W], F32) for t in range(PACK)]
+        norm2 = [sb("norm2_%d" % t, [P, W], F32) for t in range(PACK)]
+        radius = [sb("radius%d" % t, [P, W], F32) for t in range(PACK)]
+        result = [sb("result%d" % t, [P, S], F32) for t in range(PACK)]
+        rounded = [sb("rounded%d" % h, [P, HALF, PACK], BF16) for h in range(2)]
+        out_rows = out_0.rearrange("(p t) c -> p t c", t=PACK)
+
+        def fetch(t):
+            nc.vector.tensor_scalar(pairs[t][:, :W], score[t][:].indirect(n3_l[:]), -0.5, 0.0, ALU.mult, ALU.add)
+            nc.vector.tensor_copy(pairs[t][:, W:], score[t][:].indirect(n4_l[:]))
+            nc.scalar.activation(squares[t][:], pairs[t][:], ACT.Square)
+
+        def root(t):
+            nc.vector.scalar_tensor_tensor(norm2[t][:], squares[t][:, :W], 4.0, squares[t][:, W:], ALU.mult, ALU.add)
+            nc.scalar.activation(radius[t][:], norm2[t][:], ACT.Sqrt, bias=0.25)
+
+        def put_rb(t):
+            nc.vector.tensor_tensor(result[t][:].indirect(n4_l[:]), pairs[t][:, W:], pairs[t][:, :W], ALU.add)
+
+        def put_ra(t):
+            nc.vector.tensor_copy(result[t][:].indirect(n3_l[:]), radius[t][:])
+
+        def hand_out(t):
+            nc.sync.dma_start(out_rows[:, t, :], result[t][:])
+            nc.scalar.copy(rounded[0][:, :, t], result[t][:, :HALF])
+            if t < 2:
+                nc.scalar.copy(rounded[1][:, :, t], result[t][:, HALF:])
+            else:
+                nc.vector.tensor_copy(rounded[1][:, :, t], result[t][:, HALF:])
+
+        fetch(0)
+        for t in range(PACK):
+            if t + 1 < PACK:
+                fetch(t + 1)
+            root(t)
+            put_rb(t)
+            if t > 0:
+                put_ra(t - 1)
+                hand_out(t - 1)
+        put_ra(PACK - 1)
+        hand_out(PACK - 1)
+
+        words_out = out_1[0].rearrange("p c t -> p (c t)").bitcast(I32)
+        out_s = sb("out_s", [P, S], U8)
+        for h in (1, 0):
+            cols = slice(h * HALF, (h + 1) * HALF)
+            out_w = sb("out_w%d" % h, [P, HALF], U32)
+            nc.vector.quantize_mx(out_w[:].bitcast(FP8X4), out_s[:, cols], rounded[h][:].rearrange("p c t -> p (c t)"))
+            nc.sync.dma_start(words_out[:, cols], out_w[:].bitcast(I32))
+        for q in range(4):
+            nc.scalar.dma_start(out_2[0, 4 * q : 4 * q + 4, :].bitcast(I32), out_s[32 * q : 32 * q + 4, :].bitcast(I32))

@@ -1,6 +1,7 @@
 from contextlib import ExitStack
 
 import concourse.mybir as mybir
+from concourse.masks import make_identity
 
 F32 = mybir.dt.float32
 BF16 = mybir.dt.bfloat16
@@ -26,6 +27,7 @@ def tile_picked_twctriebpolar_none_po_kernel(tc, x_words, x_scales, w1_words, w1
     nc = tc.nc
     with ExitStack() as ctx:
         held = ctx.enter_context(tc.tile_pool(name="held", bufs=1))
+        placed = ctx.enter_context(tc.tile_pool(name="placed", bufs=1))
         psum = ctx.enter_context(tc.psum_pool(name="psum", bufs=8))
 
         def sb(name, shape, dtype):
@@ -45,6 +47,10 @@ def tile_picked_twctriebpolar_none_po_kernel(tc, x_words, x_scales, w1_words, w1
         w1s_raw = sb("w1s_raw", [P, S], U8)
         for tile in (xs, w2s_raw, w1s_raw):
             nc.vector.memset(tile[:].bitcast(I32), 0)
+        ident = sb("ident", [P, P], F32)
+        make_identity(nc, ident[:])
+        warm = sb("warm", [P, 1], F32)
+        nc.scalar.activation(warm[:], ident[:, 0:1], ACT.Sigmoid)
 
         xw = sb("xw", [P, T], U32)
         w2w_raw = sb("w2w_raw", [P, 2 * S], U8)
@@ -54,26 +60,26 @@ def tile_picked_twctriebpolar_none_po_kernel(tc, x_words, x_scales, w1_words, w1
         load_scales(xs, x_scales)
         two_l = load_list("two_l", two)
         nc.sync.dma_start(w2w_raw[:].bitcast(I32), w2_words[0].bitcast(I32))
+        offs_l = load_list("offs_l", offs)
         nc.sync.dma_start(xw[:].bitcast(I32), x_words[0].rearrange("p n t -> p (n t)").bitcast(I32))
         load_scales(w2s_raw, w2_scales)
-        offs_l = load_list("offs_l", offs)
         nc.sync.dma_start(w1w_raw[:].bitcast(I32), w1_words[0].bitcast(I32))
-        load_scales(w1s_raw, w1_scales)
+        cand_l = load_list("cand_l", cand)
         n2_l = load_list("n2_l", n2)
+        load_scales(w1s_raw, w1_scales)
         nc.sync.dma_start(gain[:], gs.rearrange("(p t) o -> p (t o)", t=PACK))
         n1_l = load_list("n1_l", n1)
-        cand_l = load_list("cand_l", cand)
         n3_l = load_list("n3_l", n3)
         n4_l = load_list("n4_l", n4)
 
         def deal_words(name, raw):
             dealt = sb(name, [P, 2 * S], U8)
-            nc.vector.tensor_copy(dealt[:].rearrange("p (t m b) -> p t m b", t=PACK, b=2), raw[:].rearrange("p (m t b) -> p t m b", t=PACK, b=2))
+            nc.gpsimd.tensor_copy(dealt[:].rearrange("p (t m b) -> p t m b", t=PACK, b=2), raw[:].rearrange("p (m t b) -> p t m b", t=PACK, b=2))
             return dealt
 
-        def deal_scales(name, raw):
+        def deal_scales(name, raw, engine):
             dealt = sb(name, [P, S], U8)
-            nc.vector.tensor_copy(dealt[:].rearrange("p (t m) -> p t m", t=PACK), raw[:].rearrange("p (m t) -> p t m", t=PACK))
+            engine.tensor_copy(dealt[:].rearrange("p (t m) -> p t m", t=PACK), raw[:].rearrange("p (m t) -> p t m", t=PACK))
             return dealt
 
         def pick_scales(name, offsets):
@@ -97,19 +103,24 @@ def tile_picked_twctriebpolar_none_po_kernel(tc, x_words, x_scales, w1_words, w1
                 nc.scalar.activation(windows[t ^ 1][:, S:], bank[:], ACT.Copy, scale=scale)
             return windows
 
-        two_s = pick_scales("two_s", two_l)
         w2w = deal_words("w2w", w2w_raw)
+        two_s = pick_scales("two_s", two_l)
+        offs_s = pick_scales("offs_s", offs_l)
         two_w = pick_words("two_w", two_l)
-        w2s = deal_scales("w2s", w2s_raw)
+        w2s = deal_scales("w2s", w2s_raw, nc.gpsimd)
         d_win = project("d", w2w, w2s, two_w, two_s, None)
 
         offs_w = pick_words("offs_w", offs_l)
-        offs_s = pick_scales("offs_s", offs_l)
         w1w = deal_words("w1w", w1w_raw)
-        w1s = deal_scales("w1s", w1s_raw)
+        w1s = deal_scales("w1s", w1s_raw, nc.gpsimd)
         y_win = project("y", w1w, w1s, offs_w, offs_s, gain)
 
         cand_s_raw = pick_scales("cand_s_raw", cand_l)
+        cand_w_raw = pick_words("cand_w_raw", cand_l)
+        first_w = sb("first_w", [P, P], U32)
+        first_s = sb("first_s", [P, P], U8)
+        nc.vector.tensor_copy(first_s[:], cand_s_raw[:, 0::PACK])
+        nc.vector.tensor_copy(first_w[:], cand_w_raw[:, 0::PACK])
 
         gate = sb("gate", [P, PACK, S], F32)
         ysum = sb("ysum", [P, PACK, S], F32)
@@ -117,19 +128,17 @@ def tile_picked_twctriebpolar_none_po_kernel(tc, x_words, x_scales, w1_words, w1
             dsum = sb("dsum%d" % t, [P, S], F32)
             nc.vector.tensor_tensor(dsum[:], d_win[t][:].indirect(n2_l[:]), d_win[t ^ 1][:, S:], ALU.add)
             nc.scalar.activation(gate[:, t, :], dsum[:], ACT.Sigmoid)
+        nc.scalar.activation(warm[:], gate[:, PACK - 1, 0:1], ACT.Sqrt, bias=0.25)
         for t in range(PACK):
             nc.vector.tensor_tensor(ysum[:, t, :], y_win[t][:].indirect(n1_l[:]), y_win[t ^ 1][:, S:], ALU.add)
 
-        cand_w = sb("cand_w", [P, S], U32)
-        nc.vector.tensor_copy(cand_w[:].rearrange("p (t m) -> p m t", t=PACK), xw[:].indirect(cand_l[:]))
         z_half = []
         for h in range(2):
             cols = slice(h * HALF, (h + 1) * HALF)
-            z = sb("z%d" % h, [P, HALF, PACK], BF16)
+            z = placed.tile([P, HALF, PACK], BF16, name="z%d" % h, align_bytes=64, offset=4096 + 2048 * h)
             nc.vector.tensor_tensor(z[:].rearrange("p (c i) t -> p c t i", i=4), ysum[:, :, cols].rearrange("p t (c i) -> p c t i", i=4),
                                     gate[:, :, cols].rearrange("p t (c i) -> p c t i", i=4), ALU.mult)
             z_half.append(z)
-        cand_s = deal_scales("cand_s", cand_s_raw)
         z_w = []
         z_s = []
         for h in range(2):
@@ -137,32 +146,50 @@ def tile_picked_twctriebpolar_none_po_kernel(tc, x_words, x_scales, w1_words, w1
             z_s.append(sb("z_s%d" % h, [P, HALF], U8))
             nc.vector.quantize_mx(z_w[h][:].bitcast(FP8X4), z_s[h][:], z_half[h][:].rearrange("p c t -> p (c t)"))
 
+        rest_w = placed.tile([P, PACK - 1, P], U32, name="rest_w", align_bytes=64, offset=4096 + 2048)
+        rest_s = placed.tile([P, PACK - 1, P], U8, name="rest_s", align_bytes=64, offset=4096 + 2048 + 1536)
+        nc.vector.tensor_copy(rest_s[:], cand_s_raw[:].rearrange("p (m t) -> p t m", t=PACK)[:, 1:, :])
+        nc.vector.tensor_copy(rest_w[:], cand_w_raw[:].rearrange("p (m t) -> p t m", t=PACK)[:, 1:, :])
+        cand_w = [first_w[:]] + [rest_w[:, t, :] for t in range(PACK - 1)]
+        cand_s = [first_s[:]] + [rest_s[:, t, :] for t in range(PACK - 1)]
+
         score = [sb("score%d" % t, [P, S], F32) for t in range(PACK)]
         for t in range(PACK):
             for h in range(2):
                 bank = psum.tile([P, S], F32, name="bank")
-                nc.tensor.matmul_mx(bank[:, :HALF], lhsT=cand_w[:, P * t : P * (t + 1)].bitcast(FP8X4), lhsT_scale=cand_s[:, P * t : P * (t + 1)],
+                nc.tensor.matmul_mx(bank[:, :HALF], lhsT=cand_w[t].bitcast(FP8X4), lhsT_scale=cand_s[t],
                                     rhs=z_w[h][:].bitcast(FP8X4), rhs_scale=z_s[h][:], start=True, stop=True)
                 nc.scalar.activation(score[t][:, h * HALF : (h + 1) * HALF], bank[:, :HALF], ACT.Copy, scale=0.0625)
 
         pairs = [sb("pairs%d" % t, [P, 2 * W], F32) for t in range(PACK)]
         squares = [sb("squares%d" % t, [P, 2 * W], F32) for t in range(PACK)]
-        norm2 = [sb("norm2_%d" % t, [P, W], F32) for t in range(PACK)]
+        norm2 = [sb("norm2_%d" % t, [P, W], F32) for t in range(PACK - 1)]
+        norm2.append(placed.tile([P, W], F32, name="norm2_3", align_bytes=64, offset=1536))
         radius = [sb("radius%d" % t, [P, W], F32) for t in range(PACK)]
-        result = [sb("result%d" % t, [P, S], F32) for t in range(PACK)]
-        rounded = [sb("rounded%d" % h, [P, HALF, PACK], BF16) for h in range(2)]
+        result = []
+        rounded = [placed.tile([P, HALF, PACK], BF16, name="rounded%d" % h, align_bytes=64, offset=2048 * h) for h in range(2)]
         out_rows = out_0.rearrange("(p t) c -> p t c", t=PACK)
 
         def fetch(t):
             nc.vector.tensor_scalar(pairs[t][:, :W], score[t][:].indirect(n3_l[:]), -0.5, 0.0, ALU.mult, ALU.add)
             nc.vector.tensor_copy(pairs[t][:, W:], score[t][:].indirect(n4_l[:]))
-            nc.scalar.activation(squares[t][:], pairs[t][:], ACT.Square)
+            nc.scalar.activation(squares[t][:, :W], pairs[t][:, :W], ACT.Square, scale=2.0)
+            nc.scalar.activation(squares[t][:, W:], pairs[t][:, W:], ACT.Square)
 
         def root(t):
-            nc.vector.scalar_tensor_tensor(norm2[t][:], squares[t][:, :W], 4.0, squares[t][:, W:], ALU.mult, ALU.add)
-            nc.scalar.activation(radius[t][:], norm2[t][:], ACT.Sqrt, bias=0.25)
+            turned = psum.tile([P, S], F32, name="bank")
+            for b in range(2):
+                for term in range(2):
+                    nc.tensor.matmul(turned[:, P * b : P * (b + 1)], lhsT=squares[t][:, term * W + P * b : term * W + P * (b + 1)], rhs=ident[:],
+                                     is_transpose=True, start=term == 0, stop=term == 1)
+            nc.scalar.activation(norm2[t][:], turned[:, :W], ACT.Sqrt, bias=0.25)
+            back = psum.tile([P, S], F32, name="bank")
+            for b in range(2):
+                nc.tensor.transpose(back[:, P * b : P * (b + 1)], norm2[t][:, P * b : P * (b + 1)], ident[:])
+            nc.scalar.copy(radius[t][:], back[:, :W])
 
         def put_rb(t):
+            result.append(sb(("score2", "score3", "pairs0", "pairs1")[t], [P, S], F32))
             nc.vector.tensor_tensor(result[t][:].indirect(n4_l[:]), pairs[t][:, W:], pairs[t][:, :W], ALU.add)
 
         def put_ra(t):
@@ -176,17 +203,12 @@ def tile_picked_twctriebpolar_none_po_kernel(tc, x_words, x_scales, w1_words, w1
             else:
                 nc.vector.tensor_copy(rounded[1][:, :, t], result[t][:, HALF:])
 
-        fetch(0)
+        for stage in (fetch, root, put_rb):
+            for t in range(PACK):
+                stage(t)
         for t in range(PACK):
-            if t + 1 < PACK:
-                fetch(t + 1)
-            root(t)
-            put_rb(t)
-            if t > 0:
-                put_ra(t - 1)
-                hand_out(t - 1)
-        put_ra(PACK - 1)
-        hand_out(PACK - 1)
+            put_ra(t)
+            hand_out(t)
 
         words_out = out_1[0].rearrange("p c t -> p (c t)").bitcast(I32)
         out_s = sb("out_s", [P, S], U8)
@@ -196,4 +218,4 @@ def tile_picked_twctriebpolar_none_po_kernel(tc, x_words, x_scales, w1_words, w1
             nc.vector.quantize_mx(out_w[:].bitcast(FP8X4), out_s[:, cols], rounded[h][:].rearrange("p c t -> p (c t)"))
             nc.sync.dma_start(words_out[:, cols], out_w[:].bitcast(I32))
         for q in range(4):
-            nc.scalar.dma_start(out_2[0, 4 * q : 4 * q + 4, :].bitcast(I32), out_s[32 * q : 32 * q + 4, :].bitcast(I32))
+            (nc.scalar if q % 2 else nc.sync).dma_start(out_2[0, 4 * q : 4 * q + 4, :].bitcast(I32), out_s[32 * q : 32 * q + 4, :].bitcast(I32))

@@ -20,6 +20,7 @@ T = 2048
 S = 512
 W = 256
 HALF = S // 2
+ORDER = (0, 2, 3, 1)
 FLOPS = 3 * 2 * 512 * 512 * 512
 
 
@@ -72,9 +73,9 @@ def tile_picked_twctriebpolar_none_po_kernel(tc, x_words, x_scales, w1_words, w1
         n3_l = load_list("n3_l", n3)
         n4_l = load_list("n4_l", n4)
 
-        def deal_words(name, raw):
+        def deal_words(name, raw, engine):
             dealt = sb(name, [P, 2 * S], U8)
-            nc.gpsimd.tensor_copy(dealt[:].rearrange("p (t m b) -> p t m b", t=PACK, b=2), raw[:].rearrange("p (m t b) -> p t m b", t=PACK, b=2))
+            engine.tensor_copy(dealt[:].rearrange("p (t m b) -> p t m b", t=PACK, b=2), raw[:].rearrange("p (m t b) -> p t m b", t=PACK, b=2))
             return dealt
 
         def deal_scales(name, raw, engine):
@@ -103,7 +104,7 @@ def tile_picked_twctriebpolar_none_po_kernel(tc, x_words, x_scales, w1_words, w1
                 nc.scalar.activation(windows[t ^ 1][:, S:], bank[:], ACT.Copy, scale=scale)
             return windows
 
-        w2w = deal_words("w2w", w2w_raw)
+        w2w = deal_words("w2w", w2w_raw, nc.vector)
         two_s = pick_scales("two_s", two_l)
         offs_s = pick_scales("offs_s", offs_l)
         two_w = pick_words("two_w", two_l)
@@ -111,7 +112,7 @@ def tile_picked_twctriebpolar_none_po_kernel(tc, x_words, x_scales, w1_words, w1
         d_win = project("d", w2w, w2s, two_w, two_s, None)
 
         offs_w = pick_words("offs_w", offs_l)
-        w1w = deal_words("w1w", w1w_raw)
+        w1w = deal_words("w1w", w1w_raw, nc.gpsimd)
         w1s = deal_scales("w1s", w1s_raw, nc.gpsimd)
         y_win = project("y", w1w, w1s, offs_w, offs_s, gain)
 
@@ -136,8 +137,8 @@ def tile_picked_twctriebpolar_none_po_kernel(tc, x_words, x_scales, w1_words, w1
         for h in range(2):
             cols = slice(h * HALF, (h + 1) * HALF)
             z = placed.tile([P, HALF, PACK], BF16, name="z%d" % h, align_bytes=64, offset=4096 + 2048 * h)
-            nc.vector.tensor_tensor(z[:].rearrange("p (c i) t -> p c t i", i=4), ysum[:, :, cols].rearrange("p t (c i) -> p c t i", i=4),
-                                    gate[:, :, cols].rearrange("p t (c i) -> p c t i", i=4), ALU.mult)
+            nc.vector.tensor_tensor(z[:].rearrange("p (c i) t -> p c t i", i=2), ysum[:, :, cols].rearrange("p t (c i) -> p c t i", i=2),
+                                    gate[:, :, cols].rearrange("p t (c i) -> p c t i", i=2), ALU.mult)
             z_half.append(z)
         z_w = []
         z_s = []
@@ -153,19 +154,21 @@ def tile_picked_twctriebpolar_none_po_kernel(tc, x_words, x_scales, w1_words, w1
         cand_w = [first_w[:]] + [rest_w[:, t, :] for t in range(PACK - 1)]
         cand_s = [first_s[:]] + [rest_s[:, t, :] for t in range(PACK - 1)]
 
-        score = [sb("score%d" % t, [P, S], F32) for t in range(PACK)]
-        for t in range(PACK):
+        score = [sb("score%d" % t, [P, S], F32) for t in range(PACK - 1)]
+        score.append(placed.tile([P, S], F32, name="score3", align_bytes=64, offset=8192 + 1024))
+        for k, t in enumerate(ORDER):
             for h in range(2):
                 bank = psum.tile([P, S], F32, name="bank")
                 nc.tensor.matmul_mx(bank[:, :HALF], lhsT=cand_w[t].bitcast(FP8X4), lhsT_scale=cand_s[t],
                                     rhs=z_w[h][:].bitcast(FP8X4), rhs_scale=z_s[h][:], start=True, stop=True)
-                nc.scalar.activation(score[t][:, h * HALF : (h + 1) * HALF], bank[:, :HALF], ACT.Copy, scale=0.0625)
+                nc.scalar.activation(score[k][:, h * HALF : (h + 1) * HALF], bank[:, :HALF], ACT.Copy, scale=0.0625)
 
         pairs = [sb("pairs%d" % t, [P, 2 * W], F32) for t in range(PACK)]
-        squares = [sb("squares%d" % t, [P, 2 * W], F32) for t in range(PACK)]
+        squares = []
         norm2 = [sb("norm2_%d" % t, [P, W], F32) for t in range(PACK - 1)]
         norm2.append(placed.tile([P, W], F32, name="norm2_3", align_bytes=64, offset=1536))
-        radius = [sb("radius%d" % t, [P, W], F32) for t in range(PACK)]
+        radius = []
+        backs = []
         result = []
         rounded = [placed.tile([P, HALF, PACK], BF16, name="rounded%d" % h, align_bytes=64, offset=2048 * h) for h in range(2)]
         out_rows = out_0.rearrange("(p t) c -> p t c", t=PACK)
@@ -173,8 +176,15 @@ def tile_picked_twctriebpolar_none_po_kernel(tc, x_words, x_scales, w1_words, w1
         def fetch(t):
             nc.vector.tensor_scalar(pairs[t][:, :W], score[t][:].indirect(n3_l[:]), -0.5, 0.0, ALU.mult, ALU.add)
             nc.vector.tensor_copy(pairs[t][:, W:], score[t][:].indirect(n4_l[:]))
+
+        def square(t):
+            squares.append(sb("squares%d" % (t % 2), [P, 2 * W], F32))
             nc.scalar.activation(squares[t][:, :W], pairs[t][:, :W], ACT.Square, scale=2.0)
             nc.scalar.activation(squares[t][:, W:], pairs[t][:, W:], ACT.Square)
+
+        def take_radius(t, tile):
+            radius.append(tile)
+            nc.scalar.copy(tile[:], backs[t][:, :W])
 
         def root(t):
             turned = psum.tile([P, S], F32, name="bank")
@@ -186,27 +196,42 @@ def tile_picked_twctriebpolar_none_po_kernel(tc, x_words, x_scales, w1_words, w1
             back = psum.tile([P, S], F32, name="bank")
             for b in range(2):
                 nc.tensor.transpose(back[:, P * b : P * (b + 1)], norm2[t][:, P * b : P * (b + 1)], ident[:])
-            nc.scalar.copy(radius[t][:], back[:, :W])
+            backs.append(back)
+            if t + 1 < PACK:
+                take_radius(t, sb("radius%d" % t, [P, W], F32))
 
         def put_rb(t):
-            result.append(sb(("score2", "score3", "pairs0", "pairs1")[t], [P, S], F32))
+            if t < 2:
+                result.append(placed.tile([P, S], F32, name="result%d" % t, align_bytes=64, offset=8192 + 2048 * t))
+            else:
+                result.append(sb("norm2_%d" % (t - 1), [P, S], F32))
             nc.vector.tensor_tensor(result[t][:].indirect(n4_l[:]), pairs[t][:, W:], pairs[t][:, :W], ALU.add)
 
         def put_ra(t):
             nc.vector.tensor_copy(result[t][:].indirect(n3_l[:]), radius[t][:])
 
-        def hand_out(t):
-            nc.sync.dma_start(out_rows[:, t, :], result[t][:])
-            nc.scalar.copy(rounded[0][:, :, t], result[t][:, :HALF])
-            if t < 2:
-                nc.scalar.copy(rounded[1][:, :, t], result[t][:, HALF:])
+        def hand_out(k):
+            t = ORDER[k]
+            nc.sync.dma_start(out_rows[:, t, :], result[k][:])
+            nc.scalar.copy(rounded[0][:, :, t], result[k][:, :HALF])
+            if k + 1 < PACK:
+                nc.scalar.copy(rounded[1][:, :, t], result[k][:, HALF:])
             else:
-                nc.vector.tensor_copy(rounded[1][:, :, t], result[t][:, HALF:])
+                nc.vector.tensor_copy(rounded[1][:, :, t], result[k][:, HALF:])
+            if k == 0:
+                take_radius(PACK - 1, placed.tile([P, W], F32, name="radius3", align_bytes=64, offset=8192))
 
-        for stage in (fetch, root, put_rb):
-            for t in range(PACK):
-                stage(t)
         for t in range(PACK):
+            fetch(t)
+        square(0)
+        for t in range(PACK):
+            if t + 1 < PACK:
+                square(t + 1)
+            root(t)
+        put_rb(0)
+        for t in range(PACK):
+            if t + 1 < PACK:
+                put_rb(t + 1)
             put_ra(t)
             hand_out(t)
 

@@ -16,23 +16,38 @@ ALU = mybir.AluOpType
 
 P = 128
 PACK = 4
-T = 2048
+TOKENS = 2048
 S = 512
-W = 256
+PAIRS = 256
 HALF = S // 2
-ORDER = (0, 2, 3, 1)
+QUADRANTS = 4
+PSUM_BANKS = 8
+
+TILE_ORDER = (0, 2, 3, 1)
+LAST = PACK - 1
+
+ROW = 4 * S
+ROUNDED_AT = 0
+Z_AT = 2 * ROW
+RESULT_AT = 4 * ROW
+
 FLOPS = 3 * 2 * 512 * 512 * 512
 
 
-def tile_picked_twctriebpolar_none_po_kernel(tc, x_words, x_scales, w1_words, w1_scales, w2_words, w2_scales, gs, offs, two, n1, n2, cand, n3, n4, out_0, out_1, out_2):
+def tile_picked_twctriebpolar_none_po_kernel(
+    tc, x_words, x_scales, w1_words, w1_scales, w2_words, w2_scales, gs, offs, two, n1, n2, cand, n3, n4, out_0, out_1, out_2
+):
     nc = tc.nc
     with ExitStack() as ctx:
         held = ctx.enter_context(tc.tile_pool(name="held", bufs=1))
         placed = ctx.enter_context(tc.tile_pool(name="placed", bufs=1))
-        psum = ctx.enter_context(tc.psum_pool(name="psum", bufs=8))
+        psum = ctx.enter_context(tc.psum_pool(name="psum", bufs=PSUM_BANKS))
 
         def sb(name, shape, dtype):
             return held.tile(shape, dtype, name=name, align_bytes=64)
+
+        def sb_at(name, shape, dtype, offset):
+            return placed.tile(shape, dtype, name=name, align_bytes=64, offset=offset)
 
         def load_list(name, src):
             tile = held.tile(list(src.shape), U16, name=name)
@@ -40,207 +55,237 @@ def tile_picked_twctriebpolar_none_po_kernel(tc, x_words, x_scales, w1_words, w1
             return tile
 
         def load_scales(tile, src):
-            for q in range(4):
+            for q in range(QUADRANTS):
                 nc.sync.dma_start(tile[32 * q : 32 * q + 4, :].bitcast(I32), src[0, 4 * q : 4 * q + 4, :].bitcast(I32))
 
-        xs = sb("xs", [P, T], U8)
-        w2s_raw = sb("w2s_raw", [P, S], U8)
-        w1s_raw = sb("w1s_raw", [P, S], U8)
-        for tile in (xs, w2s_raw, w1s_raw):
+        table_scales = sb("table_scales", [P, TOKENS], U8)
+        w2_scales_raw = sb("w2_scales_raw", [P, S], U8)
+        w1_scales_raw = sb("w1_scales_raw", [P, S], U8)
+        for tile in (table_scales, w2_scales_raw, w1_scales_raw):
             nc.vector.memset(tile[:].bitcast(I32), 0)
-        ident = sb("ident", [P, P], F32)
-        make_identity(nc, ident[:])
-        warm = sb("warm", [P, 1], F32)
-        nc.scalar.activation(warm[:], ident[:, 0:1], ACT.Sigmoid)
 
-        xw = sb("xw", [P, T], U32)
-        w2w_raw = sb("w2w_raw", [P, 2 * S], U8)
-        w1w_raw = sb("w1w_raw", [P, 2 * S], U8)
+        warm_in = sb("warm_in", [P, 1], F32)
+        nc.gpsimd.memset(warm_in[:], 0.0)
+        warm_out = sb("warm_out", [P, 1], F32)
+        nc.scalar.activation(warm_out[:], warm_in[:], ACT.Sigmoid)
+
+        table_words = sb("table_words", [P, TOKENS], U32)
+        w2_words_raw = sb("w2_words_raw", [P, 2 * S], U8)
+        w1_words_raw = sb("w1_words_raw", [P, 2 * S], U8)
         gain = sb("gain", [P, PACK], F32)
 
-        load_scales(xs, x_scales)
-        two_l = load_list("two_l", two)
-        nc.sync.dma_start(w2w_raw[:].bitcast(I32), w2_words[0].bitcast(I32))
-        offs_l = load_list("offs_l", offs)
-        nc.sync.dma_start(xw[:].bitcast(I32), x_words[0].rearrange("p n t -> p (n t)").bitcast(I32))
-        load_scales(w2s_raw, w2_scales)
-        nc.sync.dma_start(w1w_raw[:].bitcast(I32), w1_words[0].bitcast(I32))
-        cand_l = load_list("cand_l", cand)
-        n2_l = load_list("n2_l", n2)
-        load_scales(w1s_raw, w1_scales)
+        load_scales(table_scales, x_scales)
+        two_list = load_list("two_list", two)
+        nc.sync.dma_start(w2_words_raw[:].bitcast(I32), w2_words[0].bitcast(I32))
+        nc.sync.dma_start(w1_words_raw[:].bitcast(I32), w1_words[0].bitcast(I32))
+        offs_list = load_list("offs_list", offs)
+        nc.sync.dma_start(table_words[:].bitcast(I32), x_words[0].rearrange("p n t -> p (n t)").bitcast(I32))
+        load_scales(w2_scales_raw, w2_scales)
+        cand_list = load_list("cand_list", cand)
+        n2_list = load_list("n2_list", n2)
+        load_scales(w1_scales_raw, w1_scales)
         nc.sync.dma_start(gain[:], gs.rearrange("(p t) o -> p (t o)", t=PACK))
-        n1_l = load_list("n1_l", n1)
-        n3_l = load_list("n3_l", n3)
-        n4_l = load_list("n4_l", n4)
+        n1_list = load_list("n1_list", n1)
+        n3_list = load_list("n3_list", n3)
+        n4_list = load_list("n4_list", n4)
 
-        def deal_words(name, raw, engine):
+        def deal_weight_words(name, raw):
             dealt = sb(name, [P, 2 * S], U8)
-            engine.tensor_copy(dealt[:].rearrange("p (t m b) -> p t m b", t=PACK, b=2), raw[:].rearrange("p (m t b) -> p t m b", t=PACK, b=2))
+            nc.vector.tensor_copy(
+                dealt[:].rearrange("p (t m b) -> p t m b", t=PACK, b=2), raw[:].rearrange("p (m t b) -> p t m b", t=PACK, b=2)
+            )
             return dealt
 
-        def deal_scales(name, raw, engine):
+        def deal_weight_scales(name, raw):
             dealt = sb(name, [P, S], U8)
-            engine.tensor_copy(dealt[:].rearrange("p (t m) -> p t m", t=PACK), raw[:].rearrange("p (m t) -> p t m", t=PACK))
+            nc.gpsimd.tensor_copy(dealt[:].rearrange("p (t m) -> p t m", t=PACK), raw[:].rearrange("p (m t) -> p t m", t=PACK))
             return dealt
 
-        def pick_scales(name, offsets):
-            picked = sb(name, [P, S], U8)
-            nc.vector.tensor_copy(picked[:], xs[:].indirect(offsets[:]))
+        def pick(name, table, offsets):
+            picked = sb(name, [P, S], table.dtype)
+            nc.vector.tensor_copy(picked[:], table[:].indirect(offsets[:]))
             return picked
 
-        def pick_words(name, offsets):
-            picked = sb(name, [P, S], U32)
-            nc.vector.tensor_copy(picked[:], xw[:].indirect(offsets[:]))
-            return picked
-
-        def project(name, ww, ws, words, scales, row_scale):
-            windows = [sb("%s_win%d" % (name, t), [P, 2 * S], F32) for t in range(PACK)]
+        def project(name, weight_words, weight_scales, words, scales, row_scale):
+            windows = [sb("%s_window%d" % (name, t), [P, 2 * S], F32) for t in range(PACK)]
             for t in range(PACK):
                 bank = psum.tile([P, S], F32, name="bank")
-                nc.tensor.matmul_mx(bank[:], lhsT=ww[:, 2 * P * t : 2 * P * (t + 1)].bitcast(FP4X4), lhsT_scale=ws[:, P * t : P * (t + 1)],
-                                    rhs=words[:].bitcast(FP8X4), rhs_scale=scales[:], start=True, stop=True)
-                scale = 1.0 if row_scale is None else row_scale[:, t : t + 1]
-                nc.scalar.activation(windows[t][:, :S], bank[:], ACT.Copy, scale=scale)
-                nc.scalar.activation(windows[t ^ 1][:, S:], bank[:], ACT.Copy, scale=scale)
+                nc.tensor.matmul_mx(
+                    bank[:],
+                    lhsT=weight_words[:, 2 * P * t : 2 * P * (t + 1)].bitcast(FP4X4),
+                    lhsT_scale=weight_scales[:, P * t : P * (t + 1)],
+                    rhs=words[:].bitcast(FP8X4),
+                    rhs_scale=scales[:],
+                    start=True,
+                    stop=True,
+                )
+                targets = (windows[t][:, :S], windows[t ^ 1][:, S:])
+                for target in targets if t % 2 == 0 else reversed(targets):
+                    nc.scalar.activation(target, bank[:], ACT.Copy, scale=row_scale(t))
             return windows
 
-        w2w = deal_words("w2w", w2w_raw, nc.vector)
-        two_s = pick_scales("two_s", two_l)
-        offs_s = pick_scales("offs_s", offs_l)
-        two_w = pick_words("two_w", two_l)
-        w2s = deal_scales("w2s", w2s_raw, nc.gpsimd)
-        d_win = project("d", w2w, w2s, two_w, two_s, None)
+        def add_neighbour(out, windows, t, offsets):
+            nc.vector.tensor_tensor(out, windows[t][:].indirect(offsets[:]), windows[t ^ 1][:, S:], ALU.add)
 
-        offs_w = pick_words("offs_w", offs_l)
-        w1w = deal_words("w1w", w1w_raw, nc.gpsimd)
-        w1s = deal_scales("w1s", w1s_raw, nc.gpsimd)
-        y_win = project("y", w1w, w1s, offs_w, offs_s, gain)
+        w2_words_dealt = deal_weight_words("w2_words_dealt", w2_words_raw)
+        w1_words_dealt = deal_weight_words("w1_words_dealt", w1_words_raw)
+        identity = sb("w1_words_raw", [P, P], F32)
+        make_identity(nc, identity[:])
+        two_scales = pick("two_scales", table_scales, two_list)
+        offs_scales = pick("offs_scales", table_scales, offs_list)
+        two_words = pick("two_words", table_words, two_list)
+        w2_scales_dealt = deal_weight_scales("w2_scales_dealt", w2_scales_raw)
+        d_windows = project("d", w2_words_dealt, w2_scales_dealt, two_words, two_scales, lambda t: 1.0)
 
-        cand_s_raw = pick_scales("cand_s_raw", cand_l)
-        cand_w_raw = pick_words("cand_w_raw", cand_l)
-        first_w = sb("first_w", [P, P], U32)
-        first_s = sb("first_s", [P, P], U8)
-        nc.vector.tensor_copy(first_s[:], cand_s_raw[:, 0::PACK])
-        nc.vector.tensor_copy(first_w[:], cand_w_raw[:, 0::PACK])
+        offs_words = pick("offs_words", table_words, offs_list)
+        w1_scales_dealt = deal_weight_scales("w1_scales_dealt", w1_scales_raw)
+        y_windows = project("y", w1_words_dealt, w1_scales_dealt, offs_words, offs_scales, lambda t: gain[:, t : t + 1])
+
+        def deal_candidates(dealt, picked, parity):
+            nc.vector.tensor_copy(dealt[:], picked[:].rearrange("p (m u v) -> p v u m", u=2, v=2)[:, parity])
+
+        cand_scales = pick("cand_scales", table_scales, cand_list)
+        cand_words = pick("cand_words", table_words, cand_list)
+        even_words = sb("even_words", [P, 2, P], U32)
+        even_scales = sb("even_scales", [P, 2, P], U8)
+        deal_candidates(even_scales, cand_scales, 0)
+        deal_candidates(even_words, cand_words, 0)
 
         gate = sb("gate", [P, PACK, S], F32)
-        ysum = sb("ysum", [P, PACK, S], F32)
+        y_sum = sb("y_sum", [P, PACK, S], F32)
         for t in range(PACK):
-            dsum = sb("dsum%d" % t, [P, S], F32)
-            nc.vector.tensor_tensor(dsum[:], d_win[t][:].indirect(n2_l[:]), d_win[t ^ 1][:, S:], ALU.add)
-            nc.scalar.activation(gate[:, t, :], dsum[:], ACT.Sigmoid)
-        nc.scalar.activation(warm[:], gate[:, PACK - 1, 0:1], ACT.Sqrt, bias=0.25)
+            d_sum = sb("d_sum%d" % t, [P, S], F32)
+            add_neighbour(d_sum[:], d_windows, t, n2_list)
+            nc.scalar.activation(gate[:, t, :], d_sum[:], ACT.Sigmoid)
+        nc.scalar.activation(warm_out[:], gate[:, PACK - 1, 0:1], ACT.Sqrt, bias=0.25)
         for t in range(PACK):
-            nc.vector.tensor_tensor(ysum[:, t, :], y_win[t][:].indirect(n1_l[:]), y_win[t ^ 1][:, S:], ALU.add)
+            add_neighbour(y_sum[:, t, :], y_windows, t, n1_list)
 
-        z_half = []
+        z_halves = []
         for h in range(2):
             cols = slice(h * HALF, (h + 1) * HALF)
-            z = placed.tile([P, HALF, PACK], BF16, name="z%d" % h, align_bytes=64, offset=4096 + 2048 * h)
-            nc.vector.tensor_tensor(z[:].rearrange("p (c i) t -> p c t i", i=2), ysum[:, :, cols].rearrange("p t (c i) -> p c t i", i=2),
-                                    gate[:, :, cols].rearrange("p t (c i) -> p c t i", i=2), ALU.mult)
-            z_half.append(z)
-        z_w = []
-        z_s = []
+            z = sb_at("z%d" % h, [P, HALF, PACK], BF16, Z_AT + ROW * h)
+            nc.vector.tensor_tensor(
+                z[:].rearrange("p (c i) t -> p c t i", i=2),
+                y_sum[:, :, cols].rearrange("p t (c i) -> p c t i", i=2),
+                gate[:, :, cols].rearrange("p t (c i) -> p c t i", i=2),
+                ALU.mult,
+            )
+            z_halves.append(z)
+        z_words = []
+        z_scales = []
         for h in range(2):
-            z_w.append(sb("z_w%d" % h, [P, HALF], U32))
-            z_s.append(sb("z_s%d" % h, [P, HALF], U8))
-            nc.vector.quantize_mx(z_w[h][:].bitcast(FP8X4), z_s[h][:], z_half[h][:].rearrange("p c t -> p (c t)"))
+            z_words.append(sb("z_words%d" % h, [P, HALF], U32))
+            z_scales.append(sb("z_scales%d" % h, [P, HALF], U8))
+            nc.vector.quantize_mx(z_words[h][:].bitcast(FP8X4), z_scales[h][:], z_halves[h][:].rearrange("p c t -> p (c t)"))
 
-        rest_w = placed.tile([P, PACK - 1, P], U32, name="rest_w", align_bytes=64, offset=4096 + 2048)
-        rest_s = placed.tile([P, PACK - 1, P], U8, name="rest_s", align_bytes=64, offset=4096 + 2048 + 1536)
-        nc.vector.tensor_copy(rest_s[:], cand_s_raw[:].rearrange("p (m t) -> p t m", t=PACK)[:, 1:, :])
-        nc.vector.tensor_copy(rest_w[:], cand_w_raw[:].rearrange("p (m t) -> p t m", t=PACK)[:, 1:, :])
-        cand_w = [first_w[:]] + [rest_w[:, t, :] for t in range(PACK - 1)]
-        cand_s = [first_s[:]] + [rest_s[:, t, :] for t in range(PACK - 1)]
+        odd_words = sb_at("odd_words", [P, 2, P], U32, Z_AT + ROW)
+        odd_scales = sb_at("odd_scales", [P, 2, P], U8, Z_AT + ROW + ROW // 2)
+        deal_candidates(odd_scales, cand_scales, 1)
+        deal_candidates(odd_words, cand_words, 1)
 
-        score = [sb("score%d" % t, [P, S], F32) for t in range(PACK - 1)]
-        score.append(placed.tile([P, S], F32, name="score3", align_bytes=64, offset=8192 + 1024))
-        for k, t in enumerate(ORDER):
+        score = [sb("score%d" % step, [P, S], F32) for step in range(LAST)]
+        score.append(sb_at("last_score", [P, S], F32, RESULT_AT + ROW // 2))
+        for step, t in enumerate(TILE_ORDER):
             for h in range(2):
                 bank = psum.tile([P, S], F32, name="bank")
-                nc.tensor.matmul_mx(bank[:, :HALF], lhsT=cand_w[t].bitcast(FP8X4), lhsT_scale=cand_s[t],
-                                    rhs=z_w[h][:].bitcast(FP8X4), rhs_scale=z_s[h][:], start=True, stop=True)
-                nc.scalar.activation(score[k][:, h * HALF : (h + 1) * HALF], bank[:, :HALF], ACT.Copy, scale=0.0625)
+                nc.tensor.matmul_mx(
+                    bank[:, :HALF],
+                    lhsT=(even_words, odd_words)[t % 2][:, t // 2, :].bitcast(FP8X4),
+                    lhsT_scale=(even_scales, odd_scales)[t % 2][:, t // 2, :],
+                    rhs=z_words[h][:].bitcast(FP8X4),
+                    rhs_scale=z_scales[h][:],
+                    start=True,
+                    stop=True,
+                )
+                nc.scalar.activation(score[step][:, h * HALF : (h + 1) * HALF], bank[:, :HALF], ACT.Copy, scale=0.0625)
 
-        pairs = [sb("pairs%d" % t, [P, 2 * W], F32) for t in range(PACK)]
+        fetched = [sb("fetched%d" % step, [P, 2 * PAIRS], F32) for step in range(PACK)]
         squares = []
-        norm2 = [sb("norm2_%d" % t, [P, W], F32) for t in range(PACK - 1)]
-        norm2.append(placed.tile([P, W], F32, name="norm2_3", align_bytes=64, offset=1536))
-        radius = []
-        backs = []
+        turned_ra = [sb("turned_ra%d" % step, [P, PAIRS], F32) for step in range(LAST)]
+        turned_ra.append(sb_at("last_turned_ra", [P, PAIRS], F32, ROUNDED_AT + ROW - ROW // 4))
+        ra = []
+        ra_banks = []
         result = []
-        rounded = [placed.tile([P, HALF, PACK], BF16, name="rounded%d" % h, align_bytes=64, offset=2048 * h) for h in range(2)]
+        rounded = [sb_at("rounded%d" % h, [P, HALF, PACK], BF16, ROUNDED_AT + ROW * h) for h in range(2)]
         out_rows = out_0.rearrange("(p t) c -> p t c", t=PACK)
 
-        def fetch(t):
-            nc.vector.tensor_scalar(pairs[t][:, :W], score[t][:].indirect(n3_l[:]), -0.5, 0.0, ALU.mult, ALU.add)
-            nc.vector.tensor_copy(pairs[t][:, W:], score[t][:].indirect(n4_l[:]))
+        def fetch(step):
+            nc.vector.tensor_scalar(fetched[step][:, :PAIRS], score[step][:].indirect(n3_list[:]), -0.5, 0.0, ALU.mult, ALU.add)
+            nc.vector.tensor_copy(fetched[step][:, PAIRS:], score[step][:].indirect(n4_list[:]))
 
-        def square(t):
-            squares.append(sb("squares%d" % (t % 2), [P, 2 * W], F32))
-            nc.scalar.activation(squares[t][:, :W], pairs[t][:, :W], ACT.Square, scale=2.0)
-            nc.scalar.activation(squares[t][:, W:], pairs[t][:, W:], ACT.Square)
+        def square(step):
+            squares.append(sb("squares%d" % (step % 2), [P, 2 * PAIRS], F32))
+            nc.scalar.activation(squares[step][:, :PAIRS], fetched[step][:, :PAIRS], ACT.Square, scale=2.0)
+            nc.scalar.activation(squares[step][:, PAIRS:], fetched[step][:, PAIRS:], ACT.Square)
 
-        def take_radius(t, tile):
-            radius.append(tile)
-            nc.scalar.copy(tile[:], backs[t][:, :W])
+        def copy_ra(step, tile):
+            ra.append(tile)
+            nc.scalar.copy(tile[:], ra_banks[step][:, :PAIRS])
 
-        def root(t):
-            turned = psum.tile([P, S], F32, name="bank")
-            for b in range(2):
+        def root(step):
+            summed = psum.tile([P, S], F32, name="bank")
+            for block in range(PAIRS // P):
                 for term in range(2):
-                    nc.tensor.matmul(turned[:, P * b : P * (b + 1)], lhsT=squares[t][:, term * W + P * b : term * W + P * (b + 1)], rhs=ident[:],
-                                     is_transpose=True, start=term == 0, stop=term == 1)
-            nc.scalar.activation(norm2[t][:], turned[:, :W], ACT.Sqrt, bias=0.25)
+                    first = term * PAIRS + P * block
+                    nc.tensor.matmul(
+                        summed[:, P * block : P * (block + 1)],
+                        lhsT=squares[step][:, first : first + P],
+                        rhs=identity[:],
+                        is_transpose=True,
+                        start=term == 0,
+                        stop=term == 1,
+                    )
+            nc.scalar.activation(turned_ra[step][:], summed[:, :PAIRS], ACT.Sqrt, bias=0.25)
             back = psum.tile([P, S], F32, name="bank")
-            for b in range(2):
-                nc.tensor.transpose(back[:, P * b : P * (b + 1)], norm2[t][:, P * b : P * (b + 1)], ident[:])
-            backs.append(back)
-            if t + 1 < PACK:
-                take_radius(t, sb("radius%d" % t, [P, W], F32))
+            for block in range(PAIRS // P):
+                nc.tensor.transpose(back[:, P * block : P * (block + 1)], turned_ra[step][:, P * block : P * (block + 1)], identity[:])
+            ra_banks.append(back)
+            if step < LAST:
+                copy_ra(step, sb("ra%d" % step, [P, PAIRS], F32))
 
-        def put_rb(t):
-            if t < 2:
-                result.append(placed.tile([P, S], F32, name="result%d" % t, align_bytes=64, offset=8192 + 2048 * t))
+        def put_rb(step):
+            if step < 2:
+                result.append(sb_at("result%d" % step, [P, S], F32, RESULT_AT + ROW * step))
             else:
-                result.append(sb("norm2_%d" % (t - 1), [P, S], F32))
-            nc.vector.tensor_tensor(result[t][:].indirect(n4_l[:]), pairs[t][:, W:], pairs[t][:, :W], ALU.add)
+                result.append(sb("turned_ra%d" % (step - 1), [P, S], F32))
+            nc.vector.tensor_tensor(result[step][:].indirect(n4_list[:]), fetched[step][:, PAIRS:], fetched[step][:, :PAIRS], ALU.add)
 
-        def put_ra(t):
-            nc.vector.tensor_copy(result[t][:].indirect(n3_l[:]), radius[t][:])
+        def put_ra(step):
+            nc.vector.tensor_copy(result[step][:].indirect(n3_list[:]), ra[step][:])
 
-        def hand_out(k):
-            t = ORDER[k]
-            nc.sync.dma_start(out_rows[:, t, :], result[k][:])
-            nc.scalar.copy(rounded[0][:, :, t], result[k][:, :HALF])
-            if k + 1 < PACK:
-                nc.scalar.copy(rounded[1][:, :, t], result[k][:, HALF:])
+        def hand_out(step):
+            t = TILE_ORDER[step]
+            nc.sync.dma_start(out_rows[:, t, :], result[step][:])
+            nc.scalar.copy(rounded[0][:, :, t], result[step][:, :HALF])
+            if step < LAST:
+                nc.scalar.copy(rounded[1][:, :, t], result[step][:, HALF:])
             else:
-                nc.vector.tensor_copy(rounded[1][:, :, t], result[k][:, HALF:])
-            if k == 0:
-                take_radius(PACK - 1, placed.tile([P, W], F32, name="radius3", align_bytes=64, offset=8192))
+                nc.vector.tensor_copy(rounded[1][:, :, t], result[step][:, HALF:])
+            if step == 0:
+                copy_ra(LAST, sb_at("last_ra", [P, PAIRS], F32, RESULT_AT))
 
-        for t in range(PACK):
-            fetch(t)
+        for step in range(PACK):
+            fetch(step)
         square(0)
-        for t in range(PACK):
-            if t + 1 < PACK:
-                square(t + 1)
-            root(t)
+        for step in range(PACK):
+            if step < LAST:
+                square(step + 1)
+            root(step)
         put_rb(0)
-        for t in range(PACK):
-            if t + 1 < PACK:
-                put_rb(t + 1)
-            put_ra(t)
-            hand_out(t)
+        for step in range(PACK):
+            if step < LAST:
+                put_rb(step + 1)
+            put_ra(step)
+            hand_out(step)
 
         words_out = out_1[0].rearrange("p c t -> p (c t)").bitcast(I32)
-        out_s = sb("out_s", [P, S], U8)
+        out_scales = sb("out_scales", [P, S], U8)
         for h in (1, 0):
             cols = slice(h * HALF, (h + 1) * HALF)
-            out_w = sb("out_w%d" % h, [P, HALF], U32)
-            nc.vector.quantize_mx(out_w[:].bitcast(FP8X4), out_s[:, cols], rounded[h][:].rearrange("p c t -> p (c t)"))
-            nc.sync.dma_start(words_out[:, cols], out_w[:].bitcast(I32))
-        for q in range(4):
-            (nc.scalar if q % 2 else nc.sync).dma_start(out_2[0, 4 * q : 4 * q + 4, :].bitcast(I32), out_s[32 * q : 32 * q + 4, :].bitcast(I32))
+            out_words = sb("out_words%d" % h, [P, HALF], U32)
+            nc.vector.quantize_mx(out_words[:].bitcast(FP8X4), out_scales[:, cols], rounded[h][:].rearrange("p c t -> p (c t)"))
+            nc.sync.dma_start(words_out[:, cols], out_words[:].bitcast(I32))
+        for q in range(QUADRANTS):
+            queue = nc.scalar if q % 2 else nc.sync
+            queue.dma_start(out_2[0, 4 * q : 4 * q + 4, :].bitcast(I32), out_scales[32 * q : 32 * q + 4, :].bitcast(I32))

from contextlib import ExitStack

import concourse.mybir as mybir
from concourse.masks import make_identity

F32 = mybir.dt.float32
BF16 = mybir.dt.bfloat16
I32 = mybir.dt.int32
U32 = mybir.dt.uint32
U16 = mybir.dt.uint16
U8 = mybir.dt.uint8
FP8X4 = mybir.dt.float8_e4m3fn_x4
FP4X4 = mybir.dt.float4_e2m1fn_x4
ACT = mybir.ActivationFunctionType
ALU = mybir.AluOpType

P = 128
PACK = 4
TOKENS = 2048
S = 512
PAIRS = 256
HALF = S // 2
QUADRANTS = 4
PSUM_BANKS = 8

TILE_ORDER = (0, 2, 3, 1)
LAST = PACK - 1

ROW = 4 * S
ROUNDED_AT = 0
Z_AT = 2 * ROW
RESULT_AT = 4 * ROW

FLOPS = 3 * 2 * 512 * 512 * 512


def tile_picked_twctriebpolar_none_po_kernel(
    tc, x_words, x_scales, w1_words, w1_scales, w2_words, w2_scales, gs, offs, two, n1, n2, cand, n3, n4, out_0, out_1, out_2
):
    nc = tc.nc
    with ExitStack() as ctx:
        held = ctx.enter_context(tc.tile_pool(name="held", bufs=1))
        placed = ctx.enter_context(tc.tile_pool(name="placed", bufs=1))
        psum = ctx.enter_context(tc.psum_pool(name="psum", bufs=PSUM_BANKS))

        def sb(name, shape, dtype):
            return held.tile(shape, dtype, name=name, align_bytes=64)

        def sb_at(name, shape, dtype, offset):
            return placed.tile(shape, dtype, name=name, align_bytes=64, offset=offset)

        def load_list(name, src):
            tile = held.tile(list(src.shape), U16, name=name)
            nc.sync.dma_start(tile[:], src)
            return tile

        def load_scales(tile, src):
            for q in range(QUADRANTS):
                nc.sync.dma_start(tile[32 * q : 32 * q + 4, :].bitcast(I32), src[0, 4 * q : 4 * q + 4, :].bitcast(I32))

        table_scales = sb("table_scales", [P, TOKENS], U8)
        w2_scales_raw = sb("w2_scales_raw", [P, S], U8)
        w1_scales_raw = sb("w1_scales_raw", [P, S], U8)
        for tile in (table_scales, w2_scales_raw, w1_scales_raw):
            nc.vector.memset(tile[:].bitcast(I32), 0)

        warm_in = sb("warm_in", [P, 1], F32)
        nc.gpsimd.memset(warm_in[:], 0.0)
        warm_out = sb("warm_out", [P, 1], F32)
        nc.scalar.activation(warm_out[:], warm_in[:], ACT.Sigmoid)

        table_words = sb("table_words", [P, TOKENS], U32)
        w2_words_raw = sb("w2_words_raw", [P, 2 * S], U8)
        w1_words_raw = sb("w1_words_raw", [P, 2 * S], U8)
        gain = sb("gain", [P, PACK], F32)

        load_scales(table_scales, x_scales)
        two_list = load_list("two_list", two)
        nc.sync.dma_start(w2_words_raw[:].bitcast(I32), w2_words[0].bitcast(I32))
        nc.sync.dma_start(w1_words_raw[:].bitcast(I32), w1_words[0].bitcast(I32))
        offs_list = load_list("offs_list", offs)
        nc.sync.dma_start(table_words[:].bitcast(I32), x_words[0].rearrange("p n t -> p (n t)").bitcast(I32))
        load_scales(w2_scales_raw, w2_scales)
        cand_list = load_list("cand_list", cand)
        n2_list = load_list("n2_list", n2)
        load_scales(w1_scales_raw, w1_scales)
        nc.sync.dma_start(gain[:], gs.rearrange("(p t) o -> p (t o)", t=PACK))
        n1_list = load_list("n1_list", n1)
        n3_list = load_list("n3_list", n3)
        n4_list = load_list("n4_list", n4)

        def deal_weight_words(name, raw):
            dealt = sb(name, [P, 2 * S], U8)
            nc.vector.tensor_copy(
                dealt[:].rearrange("p (t m b) -> p t m b", t=PACK, b=2), raw[:].rearrange("p (m t b) -> p t m b", t=PACK, b=2)
            )
            return dealt

        def deal_weight_scales(name, raw):
            dealt = sb(name, [P, S], U8)
            nc.gpsimd.tensor_copy(dealt[:].rearrange("p (t m) -> p t m", t=PACK), raw[:].rearrange("p (m t) -> p t m", t=PACK))
            return dealt

        def pick(name, table, offsets):
            picked = sb(name, [P, S], table.dtype)
            nc.vector.tensor_copy(picked[:], table[:].indirect(offsets[:]))
            return picked

        def project(name, weight_words, weight_scales, words, scales, row_scale):
            windows = [sb("%s_window%d" % (name, t), [P, 2 * S], F32) for t in range(PACK)]
            for t in range(PACK):
                bank = psum.tile([P, S], F32, name="bank")
                nc.tensor.matmul_mx(
                    bank[:],
                    lhsT=weight_words[:, 2 * P * t : 2 * P * (t + 1)].bitcast(FP4X4),
                    lhsT_scale=weight_scales[:, P * t : P * (t + 1)],
                    rhs=words[:].bitcast(FP8X4),
                    rhs_scale=scales[:],
                    start=True,
                    stop=True,
                )
                targets = (windows[t][:, :S], windows[t ^ 1][:, S:])
                for target in targets if t % 2 == 0 else reversed(targets):
                    nc.scalar.activation(target, bank[:], ACT.Copy, scale=row_scale(t))
            return windows

        def add_neighbour(out, windows, t, offsets):
            nc.vector.tensor_tensor(out, windows[t][:].indirect(offsets[:]), windows[t ^ 1][:, S:], ALU.add)

        w2_words_dealt = deal_weight_words("w2_words_dealt", w2_words_raw)
        w1_words_dealt = deal_weight_words("w1_words_dealt", w1_words_raw)
        identity = sb("w1_words_raw", [P, P], F32)
        make_identity(nc, identity[:])
        two_scales = pick("two_scales", table_scales, two_list)
        offs_scales = pick("offs_scales", table_scales, offs_list)
        two_words = pick("two_words", table_words, two_list)
        w2_scales_dealt = deal_weight_scales("w2_scales_dealt", w2_scales_raw)
        d_windows = project("d", w2_words_dealt, w2_scales_dealt, two_words, two_scales, lambda t: 1.0)

        offs_words = pick("offs_words", table_words, offs_list)
        w1_scales_dealt = deal_weight_scales("w1_scales_dealt", w1_scales_raw)
        y_windows = project("y", w1_words_dealt, w1_scales_dealt, offs_words, offs_scales, lambda t: gain[:, t : t + 1])

        def deal_candidates(dealt, picked, parity):
            nc.vector.tensor_copy(dealt[:], picked[:].rearrange("p (m u v) -> p v u m", u=2, v=2)[:, parity])

        cand_scales = pick("cand_scales", table_scales, cand_list)
        cand_words = pick("cand_words", table_words, cand_list)
        even_words = sb("even_words", [P, 2, P], U32)
        even_scales = sb("even_scales", [P, 2, P], U8)
        deal_candidates(even_scales, cand_scales, 0)
        deal_candidates(even_words, cand_words, 0)

        gate = sb("gate", [P, PACK, S], F32)
        y_sum = sb("y_sum", [P, PACK, S], F32)
        for t in range(PACK):
            d_sum = sb("d_sum%d" % t, [P, S], F32)
            add_neighbour(d_sum[:], d_windows, t, n2_list)
            nc.scalar.activation(gate[:, t, :], d_sum[:], ACT.Sigmoid)
        nc.scalar.activation(warm_out[:], gate[:, PACK - 1, 0:1], ACT.Sqrt, bias=0.25)
        for t in range(PACK):
            add_neighbour(y_sum[:, t, :], y_windows, t, n1_list)

        z_halves = []
        for h in range(2):
            cols = slice(h * HALF, (h + 1) * HALF)
            z = sb_at("z%d" % h, [P, HALF, PACK], BF16, Z_AT + ROW * h)
            nc.vector.tensor_tensor(
                z[:].rearrange("p (c i) t -> p c t i", i=2),
                y_sum[:, :, cols].rearrange("p t (c i) -> p c t i", i=2),
                gate[:, :, cols].rearrange("p t (c i) -> p c t i", i=2),
                ALU.mult,
            )
            z_halves.append(z)
        z_words = []
        z_scales = []
        for h in range(2):
            z_words.append(sb("z_words%d" % h, [P, HALF], U32))
            z_scales.append(sb("z_scales%d" % h, [P, HALF], U8))
            nc.vector.quantize_mx(z_words[h][:].bitcast(FP8X4), z_scales[h][:], z_halves[h][:].rearrange("p c t -> p (c t)"))

        odd_words = sb_at("odd_words", [P, 2, P], U32, Z_AT + ROW)
        odd_scales = sb_at("odd_scales", [P, 2, P], U8, Z_AT + ROW + ROW // 2)
        deal_candidates(odd_scales, cand_scales, 1)
        deal_candidates(odd_words, cand_words, 1)

        score = [sb("score%d" % step, [P, S], F32) for step in range(LAST)]
        score.append(sb_at("last_score", [P, S], F32, RESULT_AT + ROW // 2))
        for step, t in enumerate(TILE_ORDER):
            for h in range(2):
                bank = psum.tile([P, S], F32, name="bank")
                nc.tensor.matmul_mx(
                    bank[:, :HALF],
                    lhsT=(even_words, odd_words)[t % 2][:, t // 2, :].bitcast(FP8X4),
                    lhsT_scale=(even_scales, odd_scales)[t % 2][:, t // 2, :],
                    rhs=z_words[h][:].bitcast(FP8X4),
                    rhs_scale=z_scales[h][:],
                    start=True,
                    stop=True,
                )
                nc.scalar.activation(score[step][:, h * HALF : (h + 1) * HALF], bank[:, :HALF], ACT.Copy, scale=0.0625)

        fetched = [sb("fetched%d" % step, [P, 2 * PAIRS], F32) for step in range(PACK)]
        squares = []
        turned_ra = [sb("turned_ra%d" % step, [P, PAIRS], F32) for step in range(LAST)]
        turned_ra.append(sb_at("last_turned_ra", [P, PAIRS], F32, ROUNDED_AT + ROW - ROW // 4))
        ra = []
        ra_banks = []
        result = []
        rounded = [sb_at("rounded%d" % h, [P, HALF, PACK], BF16, ROUNDED_AT + ROW * h) for h in range(2)]
        out_rows = out_0.rearrange("(p t) c -> p t c", t=PACK)

        def fetch(step):
            nc.vector.tensor_scalar(fetched[step][:, :PAIRS], score[step][:].indirect(n3_list[:]), -0.5, 0.0, ALU.mult, ALU.add)
            nc.vector.tensor_copy(fetched[step][:, PAIRS:], score[step][:].indirect(n4_list[:]))

        def square(step):
            squares.append(sb("squares%d" % (step % 2), [P, 2 * PAIRS], F32))
            nc.scalar.activation(squares[step][:, :PAIRS], fetched[step][:, :PAIRS], ACT.Square, scale=2.0)
            nc.scalar.activation(squares[step][:, PAIRS:], fetched[step][:, PAIRS:], ACT.Square)

        def copy_ra(step, tile):
            ra.append(tile)
            nc.scalar.copy(tile[:], ra_banks[step][:, :PAIRS])

        def root(step):
            summed = psum.tile([P, S], F32, name="bank")
            for block in range(PAIRS // P):
                for term in range(2):
                    first = term * PAIRS + P * block
                    nc.tensor.matmul(
                        summed[:, P * block : P * (block + 1)],
                        lhsT=squares[step][:, first : first + P],
                        rhs=identity[:],
                        is_transpose=True,
                        start=term == 0,
                        stop=term == 1,
                    )
            nc.scalar.activation(turned_ra[step][:], summed[:, :PAIRS], ACT.Sqrt, bias=0.25)
            back = psum.tile([P, S], F32, name="bank")
            for block in range(PAIRS // P):
                nc.tensor.transpose(back[:, P * block : P * (block + 1)], turned_ra[step][:, P * block : P * (block + 1)], identity[:])
            ra_banks.append(back)
            if step < LAST:
                copy_ra(step, sb("ra%d" % step, [P, PAIRS], F32))

        def put_rb(step):
            if step < 2:
                result.append(sb_at("result%d" % step, [P, S], F32, RESULT_AT + ROW * step))
            else:
                result.append(sb("turned_ra%d" % (step - 1), [P, S], F32))
            nc.vector.tensor_tensor(result[step][:].indirect(n4_list[:]), fetched[step][:, PAIRS:], fetched[step][:, :PAIRS], ALU.add)

        def put_ra(step):
            nc.vector.tensor_copy(result[step][:].indirect(n3_list[:]), ra[step][:])

        def hand_out(step):
            t = TILE_ORDER[step]
            nc.sync.dma_start(out_rows[:, t, :], result[step][:])
            nc.scalar.copy(rounded[0][:, :, t], result[step][:, :HALF])
            if step < LAST:
                nc.scalar.copy(rounded[1][:, :, t], result[step][:, HALF:])
            else:
                nc.vector.tensor_copy(rounded[1][:, :, t], result[step][:, HALF:])
            if step == 0:
                copy_ra(LAST, sb_at("last_ra", [P, PAIRS], F32, RESULT_AT))

        for step in range(PACK):
            fetch(step)
        square(0)
        for step in range(PACK):
            if step < LAST:
                square(step + 1)
            root(step)
        put_rb(0)
        for step in range(PACK):
            if step < LAST:
                put_rb(step + 1)
            put_ra(step)
            hand_out(step)

        words_out = out_1[0].rearrange("p c t -> p (c t)").bitcast(I32)
        out_scales = sb("out_scales", [P, S], U8)
        for h in (1, 0):
            cols = slice(h * HALF, (h + 1) * HALF)
            out_words = sb("out_words%d" % h, [P, HALF], U32)
            nc.vector.quantize_mx(out_words[:].bitcast(FP8X4), out_scales[:, cols], rounded[h][:].rearrange("p c t -> p (c t)"))
            nc.sync.dma_start(words_out[:, cols], out_words[:].bitcast(I32))
        for q in range(QUADRANTS):
            queue = nc.scalar if q % 2 else nc.sync
            queue.dma_start(out_2[0, 4 * q : 4 * q + 4, :].bitcast(I32), out_scales[32 * q : 32 * q + 4, :].bitcast(I32))
